import numpy as np
import ml_dtypes


def mxq(x, axis, fmt="e4m3"):
    dtype, down = {"e4m3": (ml_dtypes.float8_e4m3fn, 7), "e5m2": (ml_dtypes.float8_e5m2, 14)}[fmt]
    v = np.moveaxis(np.asarray(x, np.float32).astype(ml_dtypes.bfloat16).astype(np.float64), axis, -1)
    blocks = v.reshape(v.shape[:-1] + (-1, 32))
    amax = np.abs(blocks).max(-1, keepdims=True)
    byte = np.maximum(np.where(amax > 0, np.frexp(amax)[1] - 1 + 127, 0) - down, 1)
    scale = np.exp2(byte - 127.0)
    codes = (blocks / scale).astype(np.float32).astype(dtype).astype(np.float64)
    return np.moveaxis((codes * scale).reshape(v.shape), -1, axis)


WIDE = False


def mx_kscale(k):
    if not WIDE:
        return np.ones(k)
    levels = np.array([10, -10, 5, -5, 0])
    if k % 512:
        return np.exp2(np.random.permutation(np.resize(levels, k // 32))).repeat(32)
    a = np.empty((k // 512, 16))
    for p in range(k // 512):
        a[p, :8] = np.random.permutation(np.resize(levels, 8))
        for g in range(8):
            far = levels[np.abs(levels - a[p, g]) >= 10]
            a[p, g + 8] = far[np.random.randint(len(far))]
    return np.exp2(a.ravel()).repeat(32)


def f64(x):
    return np.asarray(x).astype(np.float64)


E2M1 = np.array([0.0, 0.5, 1.0, 1.5, 2.0, 3.0, 4.0, 6.0, -0.0, -0.5, -1.0, -1.5, -2.0, -3.0, -4.0, -6.0])


def pack_weight(w, fmt):
    k, n = w.shape
    w = f64(np.asarray(w, np.float32).astype(ml_dtypes.bfloat16)).reshape(k // 32, 32, n)
    amax = np.abs(w).max(1)
    if fmt == "e4m3":
        byte = np.frexp(amax)[1] - 1 + 127 - 7
    else:
        mant, ex = np.frexp(amax / 6.0)
        byte = np.where(mant > 0.5, ex, ex - 1) + 127
    byte = np.clip(np.where(amax > 0, byte, 1), 1, 254)
    scaled = (w * np.exp2(127.0 - byte)[:, None, :]).reshape(k, n).astype(np.float32)
    by_word = np.ascontiguousarray(scaled.reshape(k // 512, 128, 4, n).transpose(0, 1, 3, 2))
    if fmt == "e4m3":
        words = by_word.astype(ml_dtypes.float8_e4m3fn).view(np.uint8)
    else:
        c = by_word.astype(ml_dtypes.float4_e2m1fn).view(np.uint8) & 0xF
        words = (c[..., 0::2] | (c[..., 1::2] << 4)).reshape(k // 512, 128, 2 * n)
    return np.ascontiguousarray(words), np.ascontiguousarray(byte.astype(np.uint8).reshape(k // 512, 16, n))


def unpack_weight(words, scales, fmt):
    g, _, n = scales.shape
    words = np.ascontiguousarray(words).reshape(g, 128, n, -1)
    if fmt == "e4m3":
        vals = words.view(ml_dtypes.float8_e4m3fn).astype(np.float64)
    else:
        nib = np.empty((g, 128, n, 4), np.uint8)
        nib[..., 0::2] = words & 0xF
        nib[..., 1::2] = words >> 4
        vals = E2M1[nib]
    vals = vals * np.repeat(np.exp2(scales.astype(np.float64) - 127.0), 8, axis=1)[..., None]
    return vals.transpose(0, 1, 3, 2).reshape(g * 512, n)


O, K, M, T = 1024, 3072, 1536, 512


def setup_inputs():
    n = np.random.standard_normal
    s = mx_kscale(K)[:, None]
    x = n((K, T)); x[:O] *= 6.0
    w = n((K, M)) / np.sqrt(K) / s; w[:O] /= 2.0
    p_x4 = pack_weight(x[O:] * s[O:], "e2m1")
    p_w4 = pack_weight(w[O:], "e2m1")
    return {
        "x8": (x[:O] * s[:O]).astype(np.float32),
        "w8": (w[:O]).astype(np.float32),
        "x4_words": p_x4[0],
        "x4_scales": p_x4[1],
        "w4_words": p_w4[0],
        "w4_scales": p_w4[1],
        "r": (n((1536, 512))).astype(np.float32),
    }


def reference(x8, w8, x4_words, x4_scales, w4_words, w4_scales, r):
    x8_ = mxq(f64(x8), 0, "e4m3")
    w8_ = mxq(f64(w8), 0, "e4m3")
    x4_ = unpack_weight(x4_words, x4_scales, "e2m1")
    w4_ = unpack_weight(w4_words, w4_scales, "e2m1")
    y = w8_.T @ x8_ + w4_.T @ x4_
    return f64(r) + y

@@ -1,0 +1,159 @@
+from contextlib import ExitStack
+
+import concourse.mybir as mybir
+
+F32 = mybir.dt.float32
+BF16 = mybir.dt.bfloat16
+U32 = mybir.dt.uint32
+U8 = mybir.dt.uint8
+I32 = mybir.dt.int32
+FP8X4 = mybir.dt.float8_e4m3fn_x4
+FP4X4 = mybir.dt.float4_e2m1fn_x4
+
+P = 128
+T = 512
+N = 1536
+K8 = 1024
+K4 = 2048
+PASSES8 = K8 // 512
+PASSES4 = K4 // 512
+TILES = N // P
+HALF = N // 2
+BANKS = 8
+
+FLOPS = 2 * N * T * (K8 + K4)
+
+
+def tile_mix_atom_fm_res_kernel(tc, x8, w8, x4_words, x4_scales, w4_words, w4_scales, r, out):
+    nc = tc.nc
+    with ExitStack() as ctx:
+        keep = ctx.enter_context(tc.tile_pool(name="keep", bufs=1))
+        psum = ctx.enter_context(tc.psum_pool(name="psum", bufs=BANKS))
+        ctx.enter_context(tc.manual_schedule())
+
+        x_raw = [keep.tile([P, 4, T], F32, name=f"x_raw{g}", align_bytes=64) for g in range(PASSES8)]
+        w_raw0 = keep.tile([P, 4, N], F32, name="w_raw0", align_bytes=64)
+        w_raw1 = [keep.tile([P, 4, HALF], F32, name=f"w_raw1_{h}", align_bytes=64) for h in range(2)]
+        x4_w = keep.tile([P, PASSES4, 2 * T], U8, name="x4_w", align_bytes=64)
+        w4_w = keep.tile([P, PASSES4, 2 * N], U8, name="w4_w", align_bytes=64)
+        x4_s = keep.tile([P, PASSES4, T], U8, name="x4_s", align_bytes=64)
+        w4_s = keep.tile([P, PASSES4, N], U8, name="w4_s", align_bytes=64)
+        r_sb = [keep.tile([P, TILES // 2, T], F32, name=f"r_sb{h}", align_bytes=64) for h in range(2)]
+        x_grp = [keep.tile([P, T, 4], BF16, name=f"x_grp{g}", align_bytes=64) for g in range(PASSES8)]
+        w_grp = [keep.tile([P, N, 4], BF16, name=f"w_grp{g}", align_bytes=64) for g in range(PASSES8)]
+        x_q = [keep.tile([P, T], U32, name=f"x_q{g}", align_bytes=64) for g in range(PASSES8)]
+        x_s = [keep.tile([P, T], U8, name=f"x_s{g}", align_bytes=64) for g in range(PASSES8)]
+        w_q = [keep.tile([P, N], U32, name=f"w_q{g}", align_bytes=64) for g in range(PASSES8)]
+        w_s = [keep.tile([P, N], U8, name=f"w_s{g}", align_bytes=64) for g in range(PASSES8)]
+        o_sb = [keep.tile([P, T], F32, name=f"o_sb{i}", align_bytes=64) for i in range(TILES)]
+
+        x8_v = x8.rearrange("(g p j) t -> g p j t", g=PASSES8, j=4)
+        w8_v = w8.rearrange("(g p j) n -> g p j n", g=PASSES8, j=4)
+        r_v = r.rearrange("(h i p) t -> h p i t", h=2, p=P)
+        x4_scale_rows = x4_scales.bitcast(I32).rearrange("a (q s) t -> s q a t", s=4)
+        w4_scale_rows = w4_scales.bitcast(I32).rearrange("a (q s) n -> s q a n", s=4)
+
+        nc.sync.dma_start(out=x_raw[0][:], in_=x8_v[0])
+        nc.sync.dma_start(out=x_raw[1][:], in_=x8_v[1])
+        nc.sync.dma_start(out=x4_w[:].bitcast(I32), in_=x4_words.bitcast(I32).rearrange("a p b -> p a b"))
+        nc.sync.dma_start(out=w4_w[:].bitcast(I32), in_=w4_words.bitcast(I32).rearrange("a p b -> p a b"))
+        nc.sync.dma_start(out=w_raw0[:], in_=w8_v[0])
+        nc.sync.dma_start(out=w_raw1[0][:], in_=w8_v[1][:, :, 0:HALF])
+        nc.sync.dma_start(out=r_sb[0][:], in_=r_v[0])
+        nc.sync.dma_start(out=w_raw1[1][:], in_=w8_v[1][:, :, HALF:N])
+        nc.sync.dma_start(out=r_sb[1][:], in_=r_v[1])
+
+        nc.vector.memset(x4_s[:].bitcast(I32), 0)
+        nc.vector.memset(w4_s[:].bitcast(I32), 0)
+        for s in range(4):
+            nc.gpsimd.dma_start(out=x4_s[s:P:32, :, :].bitcast(I32), in_=x4_scale_rows[s])
+        for s in range(4):
+            nc.gpsimd.dma_start(out=w4_s[s:P:32, :, :].bitcast(I32), in_=w4_scale_rows[s])
+
+        for g in range(PASSES8):
+            lo, hi = slice(0, T // 2), slice(T // 2, T)
+            nc.vector.tensor_copy(out=x_grp[g][:, lo, :], in_=x_raw[g][:, :, lo].rearrange("p j t -> p t j"))
+            nc.scalar.copy(out=x_grp[g][:, hi, :], in_=x_raw[g][:, :, hi].rearrange("p j t -> p t j"))
+            nc.vector.quantize_mx(
+                out=x_q[g][:].bitcast(FP8X4), scales=x_s[g][:], in_=x_grp[g][:].rearrange("p t j -> p (t j)")
+            )
+
+        acc = {}
+
+        def cols(i):
+            return slice(i * P, (i + 1) * P)
+
+        def passes4(i):
+            acc[i] = psum.tile([P, T], F32, name="acc")
+            for a in range(PASSES4):
+                nc.tensor.matmul_mx(
+                    out=acc[i][:],
+                    lhsT=w4_w[:, a, 2 * i * P : 2 * (i + 1) * P].bitcast(FP4X4),
+                    lhsT_scale=w4_s[:, a, cols(i)],
+                    rhs=x4_w[:, a, :].bitcast(FP4X4),
+                    rhs_scale=x4_s[:, a, :],
+                    start=(a == 0),
+                    stop=False,
+                )
+
+        def pass8(g, i):
+            nc.tensor.matmul_mx(
+                out=acc[i][:],
+                lhsT=w_q[g][:, cols(i)].bitcast(FP8X4),
+                lhsT_scale=w_s[g][:, cols(i)],
+                rhs=x_q[g][:].bitcast(FP8X4),
+                rhs_scale=x_s[g][:],
+                start=False,
+                stop=(g == PASSES8 - 1),
+            )
+
+        def cast(g, i):
+            src = w_raw0[:, :, cols(i)] if g == 0 else w_raw1[i // 6][:, :, cols(i % 6)]
+            dst = w_grp[g][:, cols(i), :]
+            src = src.rearrange("p j n -> p n j")
+            if i % 2 == 0:
+                nc.vector.tensor_copy(out=dst, in_=src)
+            else:
+                nc.scalar.copy(out=dst, in_=src)
+
+        def quant(g, i):
+            nc.vector.quantize_mx(
+                out=w_q[g][:, cols(i)].bitcast(FP8X4),
+                scales=w_s[g][:, cols(i)],
+                in_=w_grp[g][:, cols(i), :].rearrange("p n j -> p (n j)"),
+            )
+
+        def prepare(g, first, last):
+            for i in range(first, last, 2):
+                cast(g, i)
+                cast(g, i + 1)
+                if i > first:
+                    quant(g, i - 2)
+                    quant(g, i - 1)
+            quant(g, last - 2)
+            quant(g, last - 1)
+
+        def finish(i):
+            nc.vector.tensor_tensor(
+                out=o_sb[i][:], in0=acc[i][:], in1=r_sb[i // 6][:, i % 6, :], op=mybir.AluOpType.add
+            )
+            nc.sync.dma_start(out=out[cols(i), :], in_=o_sb[i][:])
+
+        for i in range(BANKS):
+            passes4(i)
+        prepare(0, 0, TILES)
+        for i in range(BANKS):
+            pass8(0, i)
+        prepare(1, 0, 6)
+        for i in range(6):
+            pass8(1, i)
+        for i in range(6):
+            finish(i)
+        for i in range(BANKS, TILES):
+            passes4(i)
+            pass8(0, i)
+        prepare(1, 6, TILES)
+        for i in range(6, TILES):
+            pass8(1, i)
+        for i in range(6, TILES):
+            finish(i)

@@ -55,20 +55,20 @@ def tile_mix_atom_fm_res_kernel(tc, x8, w8, x4_words, x4_scales, w4_words, w4_sc
 
         nc.sync.dma_start(out=x_raw[0][:], in_=x8_v[0])
         nc.sync.dma_start(out=x_raw[1][:], in_=x8_v[1])
+
+        nc.vector.memset(x4_s[:].bitcast(I32), 0)
+        nc.vector.memset(w4_s[:].bitcast(I32), 0)
+        for s in range(4):
+            nc.sync.dma_start(out=x4_s[s:P:32, :, :].bitcast(I32), in_=x4_scale_rows[s])
         nc.sync.dma_start(out=x4_w[:].bitcast(I32), in_=x4_words.bitcast(I32).rearrange("a p b -> p a b"))
         nc.sync.dma_start(out=w4_w[:].bitcast(I32), in_=w4_words.bitcast(I32).rearrange("a p b -> p a b"))
+        for s in range(4):
+            nc.sync.dma_start(out=w4_s[s:P:32, :, :].bitcast(I32), in_=w4_scale_rows[s])
         nc.sync.dma_start(out=w_raw0[:], in_=w8_v[0])
         nc.sync.dma_start(out=w_raw1[0][:], in_=w8_v[1][:, :, 0:HALF])
         nc.sync.dma_start(out=r_sb[0][:], in_=r_v[0])
         nc.sync.dma_start(out=w_raw1[1][:], in_=w8_v[1][:, :, HALF:N])
         nc.sync.dma_start(out=r_sb[1][:], in_=r_v[1])
-
-        nc.vector.memset(x4_s[:].bitcast(I32), 0)
-        nc.vector.memset(w4_s[:].bitcast(I32), 0)
-        for s in range(4):
-            nc.gpsimd.dma_start(out=x4_s[s:P:32, :, :].bitcast(I32), in_=x4_scale_rows[s])
-        for s in range(4):
-            nc.gpsimd.dma_start(out=w4_s[s:P:32, :, :].bitcast(I32), in_=w4_scale_rows[s])
 
         for g in range(PASSES8):
             lo, hi = slice(0, T // 2), slice(T // 2, T)

@@ -18,8 +18,10 @@ K4 = 2048
 PASSES8 = K8 // 512
 PASSES4 = K4 // 512
 TILES = N // P
-HALF = N // 2
 BANKS = 8
+GROUP = 4
+HEAD = BANKS * P
+STORE_AFTER = {3: (0, 0, 4), 7: (1, 0, 4), 9: (2, 0, 2), 10: (2, 2, 3), 11: (2, 3, 4)}
 
 FLOPS = 2 * N * T * (K8 + K4)
 
@@ -31,25 +33,26 @@ def tile_mix_atom_fm_res_kernel(tc, x8, w8, x4_words, x4_scales, w4_words, w4_sc
         psum = ctx.enter_context(tc.psum_pool(name="psum", bufs=BANKS))
         ctx.enter_context(tc.manual_schedule())
 
-        x_raw = [keep.tile([P, 4, T], F32, name=f"x_raw{g}", align_bytes=64) for g in range(PASSES8)]
-        w_raw0 = keep.tile([P, 4, N], F32, name="w_raw0", align_bytes=64)
-        w_raw1 = [keep.tile([P, 4, HALF], F32, name=f"w_raw1_{h}", align_bytes=64) for h in range(2)]
-        x4_w = keep.tile([P, PASSES4, 2 * T], U8, name="x4_w", align_bytes=64)
-        w4_w = keep.tile([P, PASSES4, 2 * N], U8, name="w4_w", align_bytes=64)
-        x4_s = keep.tile([P, PASSES4, T], U8, name="x4_s", align_bytes=64)
-        w4_s = keep.tile([P, PASSES4, N], U8, name="w4_s", align_bytes=64)
-        r_sb = [keep.tile([P, TILES // 2, T], F32, name=f"r_sb{h}", align_bytes=64) for h in range(2)]
-        x_grp = [keep.tile([P, T, 4], BF16, name=f"x_grp{g}", align_bytes=64) for g in range(PASSES8)]
-        w_grp = [keep.tile([P, N, 4], BF16, name=f"w_grp{g}", align_bytes=64) for g in range(PASSES8)]
-        x_q = [keep.tile([P, T], U32, name=f"x_q{g}", align_bytes=64) for g in range(PASSES8)]
-        x_s = [keep.tile([P, T], U8, name=f"x_s{g}", align_bytes=64) for g in range(PASSES8)]
-        w_q = [keep.tile([P, N], U32, name=f"w_q{g}", align_bytes=64) for g in range(PASSES8)]
-        w_s = [keep.tile([P, N], U8, name=f"w_s{g}", align_bytes=64) for g in range(PASSES8)]
-        o_sb = [keep.tile([P, T], F32, name=f"o_sb{i}", align_bytes=64) for i in range(TILES)]
+        x_raw = [keep.tile([P, 4, T], F32, name=f"x_raw{g}", align_bytes=256) for g in range(PASSES8)]
+        w_raw0 = keep.tile([P, 4, N], F32, name="w_raw0", align_bytes=256)
+        w_raw1 = [keep.tile([P, 4, w], F32, name=f"w_raw1_{h}", align_bytes=256) for h, w in enumerate((HEAD, N - HEAD))]
+        x4_w = keep.tile([P, PASSES4, 2 * T], U8, name="x4_w", align_bytes=256)
+        w4_w = keep.tile([P, PASSES4, 2 * N], U8, name="w4_w", align_bytes=256)
+        x4_s = keep.tile([P, PASSES4, T], U8, name="x4_s", align_bytes=256)
+        w4_s = keep.tile([P, PASSES4, N], U8, name="w4_s", align_bytes=256)
+        r_sb = [keep.tile([P, GROUP, T], F32, name=f"r_sb{h}", align_bytes=256) for h in range(TILES // GROUP)]
+        x_grp = [keep.tile([P, T, 4], BF16, name=f"x_grp{g}", align_bytes=256) for g in range(PASSES8)]
+        w_grp = [keep.tile([P, N, 4], BF16, name=f"w_grp{g}", align_bytes=256) for g in range(PASSES8)]
+        x_q = [keep.tile([P, T], U32, name=f"x_q{g}", align_bytes=256) for g in range(PASSES8)]
+        x_s = [keep.tile([P, T], U8, name=f"x_s{g}", align_bytes=256) for g in range(PASSES8)]
+        w_q = [keep.tile([P, N], U32, name=f"w_q{g}", align_bytes=256) for g in range(PASSES8)]
+        w_s = [keep.tile([P, N], U8, name=f"w_s{g}", align_bytes=256) for g in range(PASSES8)]
+        o_sb = [keep.tile([P, GROUP, T], F32, name=f"o_sb{h}", align_bytes=256) for h in range(TILES // GROUP)]
 
         x8_v = x8.rearrange("(g p j) t -> g p j t", g=PASSES8, j=4)
         w8_v = w8.rearrange("(g p j) n -> g p j n", g=PASSES8, j=4)
-        r_v = r.rearrange("(h i p) t -> h p i t", h=2, p=P)
+        r_v = r.rearrange("(h i p) t -> h p i t", i=GROUP, p=P)
+        out_v = out.rearrange("(h i p) t -> h p i t", i=GROUP, p=P)
         x4_scale_rows = x4_scales.bitcast(I32).rearrange("a (q s) t -> s q a t", s=4)
         w4_scale_rows = w4_scales.bitcast(I32).rearrange("a (q s) n -> s q a n", s=4)
 
@@ -65,10 +68,11 @@ def tile_mix_atom_fm_res_kernel(tc, x8, w8, x4_words, x4_scales, w4_words, w4_sc
         for s in range(4):
             nc.sync.dma_start(out=w4_s[s:P:32, :, :].bitcast(I32), in_=w4_scale_rows[s])
         nc.sync.dma_start(out=w_raw0[:], in_=w8_v[0])
-        nc.sync.dma_start(out=w_raw1[0][:], in_=w8_v[1][:, :, 0:HALF])
+        nc.sync.dma_start(out=w_raw1[0][:], in_=w8_v[1][:, :, 0:HEAD])
         nc.sync.dma_start(out=r_sb[0][:], in_=r_v[0])
-        nc.sync.dma_start(out=w_raw1[1][:], in_=w8_v[1][:, :, HALF:N])
         nc.sync.dma_start(out=r_sb[1][:], in_=r_v[1])
+        nc.sync.dma_start(out=w_raw1[1][:], in_=w8_v[1][:, :, HEAD:N])
+        nc.sync.dma_start(out=r_sb[2][:], in_=r_v[2])
 
         for g in range(PASSES8):
             lo, hi = slice(0, T // 2), slice(T // 2, T)
@@ -108,7 +112,12 @@ def tile_mix_atom_fm_res_kernel(tc, x8, w8, x4_words, x4_scales, w4_words, w4_sc
             )
 
         def cast(g, i):
-            src = w_raw0[:, :, cols(i)] if g == 0 else w_raw1[i // 6][:, :, cols(i % 6)]
+            if g == 0:
+                src = w_raw0[:, :, cols(i)]
+            elif i < BANKS:
+                src = w_raw1[0][:, :, cols(i)]
+            else:
+                src = w_raw1[1][:, :, cols(i - BANKS)]
             dst = w_grp[g][:, cols(i), :]
             src = src.rearrange("p j n -> p n j")
             if i % 2 == 0:
@@ -135,25 +144,27 @@ def tile_mix_atom_fm_res_kernel(tc, x8, w8, x4_words, x4_scales, w4_words, w4_sc
 
         def finish(i):
             nc.vector.tensor_tensor(
-                out=o_sb[i][:], in0=acc[i][:], in1=r_sb[i // 6][:, i % 6, :], op=mybir.AluOpType.add
+                out=o_sb[i // GROUP][:, i % GROUP, :], in0=acc[i][:], in1=r_sb[i // GROUP][:, i % GROUP, :], op=mybir.AluOpType.add
             )
-            nc.sync.dma_start(out=out[cols(i), :], in_=o_sb[i][:])
+            if i in STORE_AFTER:
+                h, first, last = STORE_AFTER[i]
+                nc.sync.dma_start(out=out_v[h][:, first:last, :], in_=o_sb[h][:, first:last, :])
 
         for i in range(BANKS):
             passes4(i)
         prepare(0, 0, TILES)
         for i in range(BANKS):
             pass8(0, i)
-        prepare(1, 0, 6)
-        for i in range(6):
+        prepare(1, 0, BANKS)
+        for i in range(BANKS):
             pass8(1, i)
-        for i in range(6):
+        for i in range(BANKS):
             finish(i)
         for i in range(BANKS, TILES):
             passes4(i)
             pass8(0, i)
-        prepare(1, 6, TILES)
-        for i in range(6, TILES):
+        prepare(1, BANKS, TILES)
+        for i in range(BANKS, TILES):
             pass8(1, i)
-        for i in range(6, TILES):
+        for i in range(BANKS, TILES):
             finish(i)

from contextlib import ExitStack

import concourse.mybir as mybir

F32 = mybir.dt.float32
BF16 = mybir.dt.bfloat16
U32 = mybir.dt.uint32
U8 = mybir.dt.uint8
I32 = mybir.dt.int32
FP8X4 = mybir.dt.float8_e4m3fn_x4
FP4X4 = mybir.dt.float4_e2m1fn_x4

P = 128
T = 512
N = 1536
K8 = 1024
K4 = 2048
PASSES8 = K8 // 512
PASSES4 = K4 // 512
TILES = N // P
BANKS = 8
GROUP = 4
HEAD = BANKS * P
STORE_AFTER = {3: (0, 0, 4), 7: (1, 0, 4), 9: (2, 0, 2), 10: (2, 2, 3), 11: (2, 3, 4)}

FLOPS = 2 * N * T * (K8 + K4)


def tile_mix_atom_fm_res_kernel(tc, x8, w8, x4_words, x4_scales, w4_words, w4_scales, r, out):
    nc = tc.nc
    with ExitStack() as ctx:
        keep = ctx.enter_context(tc.tile_pool(name="keep", bufs=1))
        psum = ctx.enter_context(tc.psum_pool(name="psum", bufs=BANKS))
        ctx.enter_context(tc.manual_schedule())

        x_raw = [keep.tile([P, 4, T], F32, name=f"x_raw{g}", align_bytes=256) for g in range(PASSES8)]
        w_raw0 = keep.tile([P, 4, N], F32, name="w_raw0", align_bytes=256)
        w_raw1 = [keep.tile([P, 4, w], F32, name=f"w_raw1_{h}", align_bytes=256) for h, w in enumerate((HEAD, N - HEAD))]
        x4_w = keep.tile([P, PASSES4, 2 * T], U8, name="x4_w", align_bytes=256)
        w4_w = keep.tile([P, PASSES4, 2 * N], U8, name="w4_w", align_bytes=256)
        x4_s = keep.tile([P, PASSES4, T], U8, name="x4_s", align_bytes=256)
        w4_s = keep.tile([P, PASSES4, N], U8, name="w4_s", align_bytes=256)
        r_sb = [keep.tile([P, GROUP, T], F32, name=f"r_sb{h}", align_bytes=256) for h in range(TILES // GROUP)]
        x_grp = [keep.tile([P, T, 4], BF16, name=f"x_grp{g}", align_bytes=256) for g in range(PASSES8)]
        w_grp = [keep.tile([P, N, 4], BF16, name=f"w_grp{g}", align_bytes=256) for g in range(PASSES8)]
        x_q = [keep.tile([P, T], U32, name=f"x_q{g}", align_bytes=256) for g in range(PASSES8)]
        x_s = [keep.tile([P, T], U8, name=f"x_s{g}", align_bytes=256) for g in range(PASSES8)]
        w_q = [keep.tile([P, N], U32, name=f"w_q{g}", align_bytes=256) for g in range(PASSES8)]
        w_s = [keep.tile([P, N], U8, name=f"w_s{g}", align_bytes=256) for g in range(PASSES8)]
        o_sb = [keep.tile([P, GROUP, T], F32, name=f"o_sb{h}", align_bytes=256) for h in range(TILES // GROUP)]

        x8_v = x8.rearrange("(g p j) t -> g p j t", g=PASSES8, j=4)
        w8_v = w8.rearrange("(g p j) n -> g p j n", g=PASSES8, j=4)
        r_v = r.rearrange("(h i p) t -> h p i t", i=GROUP, p=P)
        out_v = out.rearrange("(h i p) t -> h p i t", i=GROUP, p=P)
        x4_scale_rows = x4_scales.bitcast(I32).rearrange("a (q s) t -> s q a t", s=4)
        w4_scale_rows = w4_scales.bitcast(I32).rearrange("a (q s) n -> s q a n", s=4)

        nc.sync.dma_start(out=x_raw[0][:], in_=x8_v[0])
        nc.sync.dma_start(out=x_raw[1][:], in_=x8_v[1])

        nc.vector.memset(x4_s[:].bitcast(I32), 0)
        nc.vector.memset(w4_s[:].bitcast(I32), 0)
        for s in range(4):
            nc.sync.dma_start(out=x4_s[s:P:32, :, :].bitcast(I32), in_=x4_scale_rows[s])
        nc.sync.dma_start(out=x4_w[:].bitcast(I32), in_=x4_words.bitcast(I32).rearrange("a p b -> p a b"))
        nc.sync.dma_start(out=w4_w[:].bitcast(I32), in_=w4_words.bitcast(I32).rearrange("a p b -> p a b"))
        for s in range(4):
            nc.sync.dma_start(out=w4_s[s:P:32, :, :].bitcast(I32), in_=w4_scale_rows[s])
        nc.sync.dma_start(out=w_raw0[:], in_=w8_v[0])
        nc.sync.dma_start(out=w_raw1[0][:], in_=w8_v[1][:, :, 0:HEAD])
        nc.sync.dma_start(out=r_sb[0][:], in_=r_v[0])
        nc.sync.dma_start(out=r_sb[1][:], in_=r_v[1])
        nc.sync.dma_start(out=w_raw1[1][:], in_=w8_v[1][:, :, HEAD:N])
        nc.sync.dma_start(out=r_sb[2][:], in_=r_v[2])

        for g in range(PASSES8):
            lo, hi = slice(0, T // 2), slice(T // 2, T)
            nc.vector.tensor_copy(out=x_grp[g][:, lo, :], in_=x_raw[g][:, :, lo].rearrange("p j t -> p t j"))
            nc.scalar.copy(out=x_grp[g][:, hi, :], in_=x_raw[g][:, :, hi].rearrange("p j t -> p t j"))
            nc.vector.quantize_mx(
                out=x_q[g][:].bitcast(FP8X4), scales=x_s[g][:], in_=x_grp[g][:].rearrange("p t j -> p (t j)")
            )

        acc = {}

        def cols(i):
            return slice(i * P, (i + 1) * P)

        def passes4(i):
            acc[i] = psum.tile([P, T], F32, name="acc")
            for a in range(PASSES4):
                nc.tensor.matmul_mx(
                    out=acc[i][:],
                    lhsT=w4_w[:, a, 2 * i * P : 2 * (i + 1) * P].bitcast(FP4X4),
                    lhsT_scale=w4_s[:, a, cols(i)],
                    rhs=x4_w[:, a, :].bitcast(FP4X4),
                    rhs_scale=x4_s[:, a, :],
                    start=(a == 0),
                    stop=False,
                )

        def pass8(g, i):
            nc.tensor.matmul_mx(
                out=acc[i][:],
                lhsT=w_q[g][:, cols(i)].bitcast(FP8X4),
                lhsT_scale=w_s[g][:, cols(i)],
                rhs=x_q[g][:].bitcast(FP8X4),
                rhs_scale=x_s[g][:],
                start=False,
                stop=(g == PASSES8 - 1),
            )

        def cast(g, i):
            if g == 0:
                src = w_raw0[:, :, cols(i)]
            elif i < BANKS:
                src = w_raw1[0][:, :, cols(i)]
            else:
                src = w_raw1[1][:, :, cols(i - BANKS)]
            dst = w_grp[g][:, cols(i), :]
            src = src.rearrange("p j n -> p n j")
            if i % 2 == 0:
                nc.vector.tensor_copy(out=dst, in_=src)
            else:
                nc.scalar.copy(out=dst, in_=src)

        def quant(g, i):
            nc.vector.quantize_mx(
                out=w_q[g][:, cols(i)].bitcast(FP8X4),
                scales=w_s[g][:, cols(i)],
                in_=w_grp[g][:, cols(i), :].rearrange("p n j -> p (n j)"),
            )

        def prepare(g, first, last):
            for i in range(first, last, 2):
                cast(g, i)
                cast(g, i + 1)
                if i > first:
                    quant(g, i - 2)
                    quant(g, i - 1)
            quant(g, last - 2)
            quant(g, last - 1)

        def finish(i):
            nc.vector.tensor_tensor(
                out=o_sb[i // GROUP][:, i % GROUP, :], in0=acc[i][:], in1=r_sb[i // GROUP][:, i % GROUP, :], op=mybir.AluOpType.add
            )
            if i in STORE_AFTER:
                h, first, last = STORE_AFTER[i]
                nc.sync.dma_start(out=out_v[h][:, first:last, :], in_=o_sb[h][:, first:last, :])

        for i in range(BANKS):
            passes4(i)
        prepare(0, 0, TILES)
        for i in range(BANKS):
            pass8(0, i)
        prepare(1, 0, BANKS)
        for i in range(BANKS):
            pass8(1, i)
        for i in range(BANKS):
            finish(i)
        for i in range(BANKS, TILES):
            passes4(i)
            pass8(0, i)
        prepare(1, BANKS, TILES)
        for i in range(BANKS, TILES):
            pass8(1, i)
        for i in range(BANKS, TILES):
            finish(i)
